import numpy as np
import ml_dtypes


def mxq(x, axis, fmt="e4m3"):
    dtype, down = {"e4m3": (ml_dtypes.float8_e4m3fn, 7), "e5m2": (ml_dtypes.float8_e5m2, 14)}[fmt]
    v = np.moveaxis(np.asarray(x, np.float32).astype(ml_dtypes.bfloat16).astype(np.float64), axis, -1)
    blocks = v.reshape(v.shape[:-1] + (-1, 32))
    amax = np.abs(blocks).max(-1, keepdims=True)
    byte = np.maximum(np.where(amax > 0, np.frexp(amax)[1] - 1 + 127, 0) - down, 1)
    scale = np.exp2(byte - 127.0)
    codes = (blocks / scale).astype(np.float32).astype(dtype).astype(np.float64)
    return np.moveaxis((codes * scale).reshape(v.shape), -1, axis)


WIDE = False


def mx_kscale(k):
    if not WIDE:
        return np.ones(k)
    levels = np.array([10, -10, 5, -5, 0])
    if k % 512:
        return np.exp2(np.random.permutation(np.resize(levels, k // 32))).repeat(32)
    a = np.empty((k // 512, 16))
    for p in range(k // 512):
        a[p, :8] = np.random.permutation(np.resize(levels, 8))
        for g in range(8):
            far = levels[np.abs(levels - a[p, g]) >= 10]
            a[p, g + 8] = far[np.random.randint(len(far))]
    return np.exp2(a.ravel()).repeat(32)


def f64(x):
    return np.asarray(x).astype(np.float64)


def striped(idx):
    return np.tile(idx.reshape(-1, 16).T, (8, 1)).astype(np.uint16)


def unstriped(offs):
    return offs[:16].T.reshape(-1).astype(np.int64)


def striped8(idx):
    return np.concatenate([x.reshape(-1, 16).T for x in idx]).astype(np.uint16)


def runs(offs, k):
    lists = np.stack([offs[16 * r : 16 * r + 16].T.reshape(-1) for r in range(8)]).astype(np.int64)
    return lists[np.arange(k) % 512 // 64]


def pack_weight(w):
    k, n = w.shape
    w = f64(np.asarray(w, np.float32).astype(ml_dtypes.bfloat16)).reshape(k // 32, 32, n)
    amax = np.abs(w).max(1)
    byte = np.clip(np.where(amax > 0, np.frexp(amax)[1] - 1 + 127 - 7, 1), 1, 254)
    scaled = (w * np.exp2(127.0 - byte)[:, None, :]).reshape(k, n).astype(np.float32)
    words = np.ascontiguousarray(scaled.reshape(k // 512, 128, 4, n).transpose(0, 1, 3, 2)).astype(ml_dtypes.float8_e4m3fn).view(np.uint8)
    return words, np.ascontiguousarray(byte.astype(np.uint8).reshape(k // 512, 16, n))


def unpack_weight(words, scales):
    g, p, n, _ = words.shape
    vals = np.ascontiguousarray(words).view(ml_dtypes.float8_e4m3fn).astype(np.float64) * np.repeat(np.exp2(scales.astype(np.float64) - 127.0), 8, axis=1)[..., None]
    return vals.transpose(0, 1, 3, 2).reshape(g * 512, n)


E2M1 = np.array([0.0, 0.5, 1.0, 1.5, 2.0, 3.0, 4.0, 6.0, -0.0, -0.5, -1.0, -1.5, -2.0, -3.0, -4.0, -6.0])


def pack_fp4(w):
    k, n = w.shape
    w = f64(np.asarray(w, np.float32).astype(ml_dtypes.bfloat16)).reshape(k // 32, 32, n)
    amax = np.abs(w).max(1)
    mant, ex = np.frexp(amax / 6.0)
    byte = np.clip(np.where(amax > 0, np.where(mant > 0.5, ex, ex - 1) + 127, 1), 1, 254)
    scaled = (w * np.exp2(127.0 - byte)[:, None, :]).reshape(k, n).astype(np.float32)
    c = np.ascontiguousarray(scaled.reshape(k // 512, 128, 4, n).transpose(0, 1, 3, 2)).astype(ml_dtypes.float4_e2m1fn).view(np.uint8) & 0xF
    words = (c[..., 0::2] | (c[..., 1::2] << 4)).reshape(k // 512, 128, 2 * n)
    return np.ascontiguousarray(words), np.ascontiguousarray(byte.astype(np.uint8).reshape(k // 512, 16, n))


def unpack_fp4(words, scales):
    g, _, n = scales.shape
    words = np.ascontiguousarray(words).reshape(g, 128, n, 2)
    nib = np.empty((g, 128, n, 4), np.uint8)
    nib[..., 0::2] = words & 0xF
    nib[..., 1::2] = words >> 4
    vals = E2M1[nib] * np.repeat(np.exp2(scales.astype(np.float64) - 127.0), 8, axis=1)[..., None]
    return vals.transpose(0, 1, 3, 2).reshape(g * 512, n)


def sigmoid(v):
    return 1.0 / (1.0 + np.exp(-np.maximum(v, -700.0)))

def planes(y):
    n, m = y.shape
    v = y.astype(np.float32).astype(ml_dtypes.bfloat16).astype(np.float64).reshape(n // 32, 32, m)
    top = np.abs(v).max(1)
    byte = np.clip(np.where(top > 0, np.frexp(top)[1] - 1 + 127 - 7, 1), 1, 254)
    codes = (v * np.exp2(127.0 - byte)[:, None, :]).reshape(n, m).astype(np.float32).astype(ml_dtypes.float8_e4m3fn).view(np.uint8)
    words = codes.reshape(n // 512, 128, 4, m).transpose(0, 1, 3, 2)
    return np.ascontiguousarray(words), np.ascontiguousarray(byte.astype(np.uint8).reshape(n // 512, 16, m))


K, T, S, N, G, H, W = 512, 2048, 512, 512, 2048, 512, 256


def setup_inputs():
    n = np.random.standard_normal
    s = mx_kscale(K)[:, None]
    u = mx_kscale(S)
    packed_xT = pack_weight(n((K, T)) * s)
    packed_dT = pack_weight(n((K, G)) / s)
    packed_w1 = pack_fp4(n((H, N)) / np.sqrt(H) / u[:, None])
    perm = np.stack([np.random.permutation(S) for _ in range(8)])
    return {
        "x_words": packed_xT[0],
        "x_scales": packed_xT[1],
        "d_words": packed_dT[0],
        "d_scales": packed_dT[1],
        "gn": (np.random.uniform(0.5, 1.5, (H, 1)) * u[:, None]).astype(np.float32),
        "w1_words": packed_w1[0],
        "w1_scales": packed_w1[1],
        "offs": striped(np.random.permutation(T)[:S]),
        "k1": striped8(np.random.randint(0, G, (8, H))),
        "n1": striped8(np.stack([np.random.permutation(S) for _ in range(8)])),
        "n2": striped8(perm[:, :W]),
        "n3": striped8(perm[:, W:]),
    }


def reference(x_words, x_scales, d_words, d_scales, gn, w1_words, w1_scales, offs, k1, n1, n2, n3):
    d_k1 = unpack_weight(d_words, d_scales)[np.arange(K)[:, None], runs(k1, K)]
    xq = unpack_weight(x_words, x_scales)[:, unstriped(offs)]
    h = 0.0625 * (d_k1.T @ xq)
    z = f64(gn) * (h * (sigmoid(h[np.arange(H)[:, None], runs(n1, H)])))
    h2 = unpack_fp4(w1_words, w1_scales).T @ mxq(z, 0, "e4m3")
    pb = h2[np.arange(N)[:, None], runs(n3, N)]
    pa = h2[np.arange(N)[:, None], runs(n2, N)]
    rb = pb - (0.5 * pa)
    ra = np.sqrt((pa) ** 2 + (pb) ** 2 + 0.25)
    ds = np.zeros((N, S))
    ds[np.arange(N)[:, None], runs(n2, N)] = ra
    out = ds.copy()
    out[np.arange(N)[:, None], runs(n3, N)] = rb
    return (out,) + planes(out)

@@ -1,0 +1,211 @@
+from contextlib import ExitStack
+
+import concourse.mybir as mybir
+
+F32 = mybir.dt.float32
+BF16 = mybir.dt.bfloat16
+I32 = mybir.dt.int32
+U32 = mybir.dt.uint32
+U16 = mybir.dt.uint16
+U8 = mybir.dt.uint8
+FP8X4 = mybir.dt.float8_e4m3fn_x4
+FP4X4 = mybir.dt.float4_e2m1fn_x4
+ACT = mybir.ActivationFunctionType
+ALU = mybir.AluOpType
+
+P = 128
+T = 2048
+S = 512
+HALF = 256
+FLOPS = 2 * 2 * 512 * 512 * 512
+
+
+def tile_picked_pqlaygatepolar_none_po_kernel(
+    tc, x_words, x_scales, d_words, d_scales, gn, w1_words, w1_scales, offs, k1, n1, n2, n3, out_0, out_1, out_2
+):
+    nc = tc.nc
+    with ExitStack() as ctx:
+        lists = ctx.enter_context(tc.tile_pool(name="lists", bufs=1))
+        keep = ctx.enter_context(tc.tile_pool(name="keep", bufs=1))
+        psum = ctx.enter_context(tc.psum_pool(name="psum", bufs=1))
+
+        k1_t = lists.tile([P, S // 16], U16, name="k1_t")
+        offs_t = lists.tile([P, S // 16], U16, name="offs_t")
+        n1_t = lists.tile([P, S // 16], U16, name="n1_t")
+        n2_t = lists.tile([P, HALF // 16], U16, name="n2_t")
+        n3_t = lists.tile([P, HALF // 16], U16, name="n3_t")
+
+        ds_win = keep.tile([P, T], U8, name="ds_win", tag="ds_win", align_bytes=64)
+        xs_win = keep.tile([P, T], U8, name="xs_win", tag="xs_win", align_bytes=64)
+        dw_win = keep.tile([P, T], I32, name="dw_win", tag="dw_win", align_bytes=64)
+        xw_win = keep.tile([P, T], I32, name="xw_win", align_bytes=64)
+        gain = keep.tile([P, 4], F32, name="gain")
+        gain16 = keep.tile([P, 4], F32, name="gain16")
+        quarter = keep.tile([P, 1], F32, name="quarter")
+
+        nc.gpsimd.memset(ds_win[:].bitcast(I32), 0)
+        nc.vector.memset(xs_win[:].bitcast(I32), 0)
+        nc.sync.dma_start(k1_t[:], k1)
+        nc.sync.dma_start(ds_win[0:P:8, :].bitcast(I32), d_scales[0].bitcast(I32))
+        nc.sync.dma_start(offs_t[:], offs)
+        nc.sync.dma_start(xs_win[0:P:8, :].bitcast(I32), x_scales[0].bitcast(I32))
+        nc.sync.dma_start(n1_t[:], n1)
+        nc.sync.dma_start(dw_win[:], d_words[0].rearrange("p n t -> p (n t)").bitcast(I32))
+        nc.sync.dma_start(xw_win[:], x_words[0].rearrange("p n t -> p (n t)").bitcast(I32))
+        nc.sync.dma_start(n2_t[:], n2)
+        nc.sync.dma_start(n3_t[:], n3)
+        nc.gpsimd.dma_start(gain[:], gn.rearrange("(p t) o -> p (t o)", t=4))
+        nc.gpsimd.memset(quarter[:], 0.25)
+        nc.gpsimd.tensor_scalar(gain16[:], gain[:], 0.0625, 0.0, ALU.mult, ALU.add)
+
+        ds_got = keep.tile([P, S], U8, name="ds_got", align_bytes=64)
+        xs_got = keep.tile([P, S], U8, name="xs_got", tag="got", align_bytes=64)
+        planes = keep.tile([P, 2 * S], U8, name="planes", align_bytes=64)
+        nc.vector.tensor_copy(ds_got[:], ds_win[:].indirect(k1_t[:]))
+        nc.vector.tensor_copy(xs_got[:], xs_win[:].indirect(offs_t[:]))
+        nc.vector.tensor_copy(
+            planes[:, 0:S].rearrange("p (t m) -> p t m", t=4), ds_got[:].rearrange("p (m t) -> p t m", t=4)
+        )
+        nc.vector.tensor_copy(planes[:, S : 2 * S].bitcast(I32), xs_got[:].bitcast(I32))
+        for c in range(1, 4):
+            nc.scalar.dma_start(planes[c:P:32, :].bitcast(I32), planes[8 * c : P : 32, :].bitcast(I32))
+
+        dw_got = keep.tile([P, S], U32, name="dw_got", tag="got", align_bytes=64)
+        dw_dealt = keep.tile([P, S], U32, name="dw_dealt", align_bytes=64)
+        nc.vector.tensor_copy(dw_got[:], dw_win[:].bitcast(U32).indirect(k1_t[:]))
+        nc.vector.tensor_copy(
+            dw_dealt[:].rearrange("p (t m) -> p t m", t=4), dw_got[:].rearrange("p (m t) -> p t m", t=4)
+        )
+
+        xw_got = [keep.tile([P, HALF], U32, name="xw_got%d" % u, align_bytes=64) for u in range(2)]
+        h_win = [keep.tile([P, S], F32, name="h_win%d" % t, align_bytes=64) for t in range(4)]
+        acc1 = {}
+        for u in range(2):
+            nc.vector.tensor_copy(xw_got[u][:], xw_win[:].bitcast(U32).indirect(offs_t[:, 16 * u : 16 * (u + 1)]))
+        for t, u in [(0, 0), (1, 0), (0, 1), (1, 1), (2, 0), (2, 1), (3, 0), (3, 1)]:
+            acc = psum.tile([P, HALF], F32, name="acc1_%d_%d" % (t, u), tag="bank%d" % (2 * t + u))
+            acc1[t, u] = acc
+            nc.tensor.matmul_mx(
+                out=acc[:],
+                lhsT=dw_dealt[:, P * t : P * (t + 1)].bitcast(FP8X4),
+                lhsT_scale=planes[:, P * t : P * (t + 1)],
+                rhs=xw_got[u][:].bitcast(FP8X4),
+                rhs_scale=planes[:, S + HALF * u : S + HALF * (u + 1)],
+                start=True,
+                stop=True,
+            )
+            dst = h_win[t][:, HALF * u : HALF * (u + 1)]
+            if t == 0:
+                nc.scalar.activation(dst, acc[:], ACT.Sigmoid, scale=0.0625)
+            elif t == 1 or u == 1:
+                nc.vector.tensor_copy(dst, acc[:])
+            else:
+                nc.scalar.copy(dst, acc[:])
+
+        ww_raw = keep.tile([P, 2 * S], U8, name="ww_raw", tag="dw_win", align_bytes=64)
+        ws_raw = keep.tile([P, S], U8, name="ws_raw", tag="xs_win", align_bytes=64)
+        ww_dealt = keep.tile([P, 2 * S], U8, name="ww_dealt", align_bytes=64)
+        ws_dealt = keep.tile([P, S], U8, name="ws_dealt", align_bytes=64)
+        nc.gpsimd.memset(ws_raw[:].bitcast(I32), 0)
+        nc.sync.dma_start(ww_raw[:].bitcast(I32), w1_words[0].bitcast(I32))
+        for q in range(4):
+            nc.sync.dma_start(
+                ws_raw[32 * q : 32 * q + 4, :].bitcast(I32), w1_scales[0, 4 * q : 4 * q + 4, :].bitcast(I32)
+            )
+        nc.gpsimd.tensor_copy(
+            ww_dealt[:].rearrange("p (t m b) -> p t m b", t=4, b=2),
+            ww_raw[:].rearrange("p (m t b) -> p t m b", t=4, b=2),
+        )
+        nc.gpsimd.tensor_copy(
+            ws_dealt[:].rearrange("p (t m) -> p t m", t=4), ws_raw[:].rearrange("p (m t) -> p t m", t=4)
+        )
+
+        h2_win = [keep.tile([P, S], F32, name="h2_win%d" % t, align_bytes=64) for t in range(4)]
+        acc2 = {}
+        for u in range(2):
+            z_rows = keep.tile([P, 4, HALF], BF16, name="z_rows%d" % u, align_bytes=64)
+            for t in range(4):
+                gate = keep.tile([P, HALF], F32, name="gate%d_%d" % (t, u), tag="gate%d" % (t if t > 0 else 4 * u), align_bytes=64)
+                picked = h_win[t][:].indirect(n1_t[:, 16 * u : 16 * (u + 1)])
+                if t == 0:
+                    nc.vector.tensor_copy(gate[:], picked)
+                else:
+                    nc.scalar.activation(gate[:], picked, ACT.Sigmoid, scale=0.0625)
+                nc.vector.scalar_tensor_tensor(
+                    z_rows[:, t, :], acc1[t, u][:], gain16[:, t : t + 1], gate[:], ALU.mult, ALU.mult
+                )
+            z_grouped = keep.tile([P, HALF, 4], BF16, name="z_grouped%d" % u, align_bytes=64)
+            z_codes = keep.tile([P, HALF], U32, name="z_codes%d" % u, align_bytes=64)
+            z_scales = keep.tile([P, HALF], U8, name="z_scales%d" % u, align_bytes=64)
+            nc.vector.tensor_copy(
+                z_grouped[:].rearrange("p (c i) t -> p c t i", i=4),
+                z_rows[:].rearrange("p t (c i) -> p c t i", i=4),
+            )
+            nc.vector.quantize_mx(
+                out=z_codes[:].bitcast(FP8X4), scales=z_scales[:], in_=z_grouped[:].rearrange("p c t -> p (c t)")
+            )
+            for t in range(4):
+                acc = psum.tile([P, HALF], F32, name="acc2_%d_%d" % (t, u), tag="bank%d" % (2 * t + u))
+                acc2[t, u] = acc
+                nc.tensor.matmul_mx(
+                    out=acc[:],
+                    lhsT=ww_dealt[:, 2 * P * t : 2 * P * (t + 1)].bitcast(FP4X4),
+                    lhsT_scale=ws_dealt[:, P * t : P * (t + 1)],
+                    rhs=z_codes[:].bitcast(FP8X4),
+                    rhs_scale=z_scales[:],
+                    start=True,
+                    stop=True,
+                )
+                if u == 0:
+                    nc.scalar.copy(h2_win[t][:, 0:HALF], acc[:])
+
+        out_rows = out_0.rearrange("(p t) c -> p t c", t=4)
+        y_rows = keep.tile([P, 4, S], BF16, name="y_rows", align_bytes=64)
+        y_wins = []
+        for t in range(4):
+            if t == 0:
+                nc.vector.tensor_copy(h2_win[t][:, HALF:S], acc2[t, 1][:])
+            else:
+                nc.scalar.copy(h2_win[t][:, HALF:S], acc2[t, 1][:])
+            pair = keep.tile([P, S], F32, name="pair%d" % t, align_bytes=64)
+            squares = keep.tile([P, S], F32, name="squares%d" % t, tag="squares%d" % t, align_bytes=64)
+            total = keep.tile([P, HALF], F32, name="total%d" % t, align_bytes=64)
+            root = keep.tile([P, HALF], F32, name="root%d" % t, align_bytes=64)
+            nc.scalar.activation(pair[:, 0:HALF], h2_win[t][:].indirect(n2_t[:]), ACT.Copy, scale=-0.5)
+            if t == 0:
+                nc.vector.tensor_copy(pair[:, HALF:S], h2_win[t][:].indirect(n3_t[:]))
+            else:
+                nc.scalar.activation(pair[:, HALF:S], h2_win[t][:].indirect(n3_t[:]), ACT.Copy)
+            nc.scalar.activation(squares[:], pair[:], ACT.Square)
+            nc.vector.scalar_tensor_tensor(
+                total[:], squares[:, 0:HALF], 4.0, squares[:, HALF:S], ALU.mult, ALU.add
+            )
+            y_win = keep.tile([P, S], F32, name="y_win%d" % t, tag="squares%d" % t, align_bytes=64)
+            y_wins.append(y_win)
+            nc.vector.tensor_tensor(y_win[:].indirect(n3_t[:]), pair[:, 0:HALF], pair[:, HALF:S], ALU.add)
+            nc.scalar.activation(root[:], total[:], ACT.Sqrt, bias=quarter[:])
+            nc.vector.tensor_copy(y_win[:].indirect(n2_t[:]), root[:])
+            nc.sync.dma_start(out_rows[:, t, :], y_win[:])
+        for t in range(3):
+            nc.scalar.copy(y_rows[:, t, :], y_wins[t][:])
+
+        y_grouped = keep.tile([P, S, 4], BF16, name="y_grouped", align_bytes=64)
+        y_codes = keep.tile([P, S], U32, name="y_codes", align_bytes=64)
+        y_scales = keep.tile([P, S], U8, name="y_scales", align_bytes=64)
+        nc.scalar.copy(y_grouped[:, 0:HALF, 0:2], y_rows[:, 0:2, 0:HALF].rearrange("p t c -> p c t"))
+        nc.scalar.copy(y_grouped[:, HALF:S, 0:3], y_rows[:, 0:3, HALF:S].rearrange("p t c -> p c t"))
+        nc.vector.tensor_copy(y_rows[:, 3, 0:HALF], y_wins[3][:, 0:HALF])
+        nc.scalar.copy(y_grouped[:, HALF:S, 3], y_wins[3][:, HALF:S])
+        nc.vector.tensor_copy(y_grouped[:, 0:HALF, 2:4], y_rows[:, 2:4, 0:HALF].rearrange("p t c -> p c t"))
+        words_out = out_1[0].rearrange("p n t -> p (n t)").bitcast(I32)
+        for u in range(2):
+            cols = slice(HALF * u, HALF * (u + 1))
+            nc.vector.quantize_mx(
+                out=y_codes[:, cols].bitcast(FP8X4),
+                scales=y_scales[:, cols],
+                in_=y_grouped[:, cols, :].rearrange("p c t -> p (c t)"),
+            )
+            nc.sync.dma_start(words_out[:, cols], y_codes[:, cols].bitcast(I32))
+        for q in range(4):
+            eng = nc.scalar if q % 2 == 0 else nc.sync
+            eng.dma_start(out_2[0, 4 * q : 4 * q + 4, :].bitcast(I32), y_scales[32 * q : 32 * q + 4, :].bitcast(I32))

@@ -79,14 +79,12 @@ def tile_picked_pqlaygatepolar_none_po_kernel(
 
         xw_got = [keep.tile([P, HALF], U32, name="xw_got%d" % u, align_bytes=64) for u in range(2)]
         h_win = [keep.tile([P, S], F32, name="h_win%d" % t, align_bytes=64) for t in range(4)]
-        acc1 = {}
+        acc1 = [psum.tile([P, S], F32, name="acc1_%d" % t, tag="bank%d" % t) for t in range(4)]
         for u in range(2):
             nc.vector.tensor_copy(xw_got[u][:], xw_win[:].bitcast(U32).indirect(offs_t[:, 16 * u : 16 * (u + 1)]))
         for t, u in [(0, 0), (1, 0), (0, 1), (1, 1), (2, 0), (2, 1), (3, 0), (3, 1)]:
-            acc = psum.tile([P, HALF], F32, name="acc1_%d_%d" % (t, u), tag="bank%d" % (2 * t + u))
-            acc1[t, u] = acc
             nc.tensor.matmul_mx(
-                out=acc[:],
+                out=acc1[t][:, HALF * u : HALF * (u + 1)],
                 lhsT=dw_dealt[:, P * t : P * (t + 1)].bitcast(FP8X4),
                 lhsT_scale=planes[:, P * t : P * (t + 1)],
                 rhs=xw_got[u][:].bitcast(FP8X4),
@@ -94,13 +92,12 @@ def tile_picked_pqlaygatepolar_none_po_kernel(
                 start=True,
                 stop=True,
             )
-            dst = h_win[t][:, HALF * u : HALF * (u + 1)]
-            if t == 0:
-                nc.scalar.activation(dst, acc[:], ACT.Sigmoid, scale=0.0625)
-            elif t == 1 or u == 1:
-                nc.vector.tensor_copy(dst, acc[:])
-            else:
-                nc.scalar.copy(dst, acc[:])
+            if u == 1 and t == 0:
+                nc.scalar.activation(h_win[t][:], acc1[t][:], ACT.Sigmoid, scale=0.0625)
+            elif u == 1 and t == 1:
+                nc.vector.tensor_copy(h_win[t][:], acc1[t][:])
+            elif u == 1:
+                nc.scalar.copy(h_win[t][:], acc1[t][:])
 
         ww_raw = keep.tile([P, 2 * S], U8, name="ww_raw", tag="dw_win", align_bytes=64)
         ws_raw = keep.tile([P, S], U8, name="ws_raw", tag="xs_win", align_bytes=64)
@@ -120,23 +117,35 @@ def tile_picked_pqlaygatepolar_none_po_kernel(
             ws_dealt[:].rearrange("p (t m) -> p t m", t=4), ws_raw[:].rearrange("p (m t) -> p t m", t=4)
         )
 
-        h2_win = [keep.tile([P, S], F32, name="h2_win%d" % t, align_bytes=64) for t in range(4)]
-        acc2 = {}
-        for u in range(2):
-            z_rows = keep.tile([P, 4, HALF], BF16, name="z_rows%d" % u, align_bytes=64)
+        h2_win = [keep.tile([P, S], F32, name="h2_win%d" % t, tag="h2_win%d" % t, align_bytes=64) for t in range(3)]
+        chunks = [(0, 256), (256, 384), (384, 512)]
+        early = {}
+        late = {}
+        for c, (lo, hi) in enumerate(chunks):
+            n = hi - lo
+            z_rows = keep.tile([P, 4, n], BF16, name="z_rows%d" % c, align_bytes=64)
             for t in range(4):
-                gate = keep.tile([P, HALF], F32, name="gate%d_%d" % (t, u), tag="gate%d" % (t if t > 0 else 4 * u), align_bytes=64)
-                picked = h_win[t][:].indirect(n1_t[:, 16 * u : 16 * (u + 1)])
+                tag = "gate%d" % t if t > 0 else "gate0_%d" % c
+                gate = keep.tile([P, n], F32, name="gate%d_%d" % (t, c), tag=tag, align_bytes=64)
+                picked = h_win[t][:].indirect(n1_t[:, lo // 16 : hi // 16])
                 if t == 0:
                     nc.vector.tensor_copy(gate[:], picked)
                 else:
                     nc.scalar.activation(gate[:], picked, ACT.Sigmoid, scale=0.0625)
                 nc.vector.scalar_tensor_tensor(
-                    z_rows[:, t, :], acc1[t, u][:], gain16[:, t : t + 1], gate[:], ALU.mult, ALU.mult
+                    z_rows[:, t, :],
+                    acc1[t][:, lo:hi],
+                    gain16[:, t : t + 1],
+                    gate[:],
+                    ALU.mult,
+                    ALU.mult,
                 )
-            z_grouped = keep.tile([P, HALF, 4], BF16, name="z_grouped%d" % u, align_bytes=64)
-            z_codes = keep.tile([P, HALF], U32, name="z_codes%d" % u, align_bytes=64)
-            z_scales = keep.tile([P, HALF], U8, name="z_scales%d" % u, align_bytes=64)
+            if c == 2:
+                warm = keep.tile([P, 1], F32, name="warm")
+                nc.scalar.activation(warm[:], gate[:, 0:1], ACT.Sqrt, bias=quarter[:])
+            z_grouped = keep.tile([P, n, 4], BF16, name="z_grouped%d" % c, align_bytes=64)
+            z_codes = keep.tile([P, n], U32, name="z_codes%d" % c, align_bytes=64)
+            z_scales = keep.tile([P, n], U8, name="z_scales%d" % c, align_bytes=64)
             nc.vector.tensor_copy(
                 z_grouped[:].rearrange("p (c i) t -> p c t i", i=4),
                 z_rows[:].rearrange("p t (c i) -> p c t i", i=4),
@@ -145,10 +154,12 @@ def tile_picked_pqlaygatepolar_none_po_kernel(
                 out=z_codes[:].bitcast(FP8X4), scales=z_scales[:], in_=z_grouped[:].rearrange("p c t -> p (c t)")
             )
             for t in range(4):
-                acc = psum.tile([P, HALF], F32, name="acc2_%d_%d" % (t, u), tag="bank%d" % (2 * t + u))
-                acc2[t, u] = acc
+                if c == 0:
+                    early[t] = psum.tile([P, S], F32, name="early%d" % t, tag="bank%d" % (4 + t))
+                if c == 2 and t < 3:
+                    late[t] = psum.tile([P, n], F32, name="late%d" % t, tag="bank%d" % t)
                 nc.tensor.matmul_mx(
-                    out=acc[:],
+                    out=early[t][:, lo:hi] if c < 2 or t == 3 else late[t][:],
                     lhsT=ww_dealt[:, 2 * P * t : 2 * P * (t + 1)].bitcast(FP4X4),
                     lhsT_scale=ws_dealt[:, P * t : P * (t + 1)],
                     rhs=z_codes[:].bitcast(FP8X4),
@@ -156,44 +167,65 @@ def tile_picked_pqlaygatepolar_none_po_kernel(
                     start=True,
                     stop=True,
                 )
-                if u == 0:
-                    nc.scalar.copy(h2_win[t][:, 0:HALF], acc[:])
+                if c == 1 and t < 2:
+                    nc.scalar.copy(h2_win[t][:, 0:384], early[t][:, 0:384])
 
         out_rows = out_0.rearrange("(p t) c -> p t c", t=4)
         y_rows = keep.tile([P, 4, S], BF16, name="y_rows", align_bytes=64)
         y_wins = []
+        totals = []
+
+        def finish(t, tag):
+            root = keep.tile([P, HALF], F32, name="root%d" % t, tag=tag, align_bytes=64)
+            nc.scalar.activation(root[:], totals[t][:], ACT.Sqrt, bias=quarter[:])
+            nc.vector.tensor_copy(y_wins[t][:].indirect(n2_t[:]), root[:])
+            nc.sync.dma_start(out_rows[:, t, :], y_wins[t][:])
+
+        nc.vector.tensor_copy(h2_win[2][:, 0:384], early[2][:, 0:384])
+        for t in range(2):
+            nc.vector.tensor_copy(h2_win[t][:, 384:S], late[t][:])
         for t in range(4):
-            if t == 0:
-                nc.vector.tensor_copy(h2_win[t][:, HALF:S], acc2[t, 1][:])
-            else:
-                nc.scalar.copy(h2_win[t][:, HALF:S], acc2[t, 1][:])
+            if t == 3:
+                h2_win.append(keep.tile([P, S], F32, name="h2_win3", tag="h2_win0", align_bytes=64))
+                nc.scalar.copy(h2_win[3][:], early[3][:])
             pair = keep.tile([P, S], F32, name="pair%d" % t, align_bytes=64)
-            squares = keep.tile([P, S], F32, name="squares%d" % t, tag="squares%d" % t, align_bytes=64)
             total = keep.tile([P, HALF], F32, name="total%d" % t, align_bytes=64)
-            root = keep.tile([P, HALF], F32, name="root%d" % t, align_bytes=64)
+            totals.append(total)
             nc.scalar.activation(pair[:, 0:HALF], h2_win[t][:].indirect(n2_t[:]), ACT.Copy, scale=-0.5)
             if t == 0:
                 nc.vector.tensor_copy(pair[:, HALF:S], h2_win[t][:].indirect(n3_t[:]))
+                nc.vector.tensor_copy(h2_win[2][:, 384:S], late[2][:])
             else:
                 nc.scalar.activation(pair[:, HALF:S], h2_win[t][:].indirect(n3_t[:]), ACT.Copy)
-            nc.scalar.activation(squares[:], pair[:], ACT.Square)
-            nc.vector.scalar_tensor_tensor(
-                total[:], squares[:, 0:HALF], 4.0, squares[:, HALF:S], ALU.mult, ALU.add
-            )
-            y_win = keep.tile([P, S], F32, name="y_win%d" % t, tag="squares%d" % t, align_bytes=64)
+            if t < 3:
+                squares = keep.tile([P, S], F32, name="squares%d" % t, align_bytes=64)
+                nc.scalar.activation(squares[:], pair[:], ACT.Square)
+                y_win = keep.tile([P, S], F32, name="y_win%d" % t, align_bytes=64)
+                nc.vector.tensor_tensor(y_win[:].indirect(n3_t[:]), pair[:, 0:HALF], pair[:, HALF:S], ALU.add)
+                nc.vector.scalar_tensor_tensor(
+                    total[:], squares[:, 0:HALF], 4.0, squares[:, HALF:S], ALU.mult, ALU.add
+                )
+            else:
+                sq_a = keep.tile([P, HALF], F32, name="sq_a", tag="sq_a", align_bytes=64)
+                sq_b = keep.tile([P, HALF], F32, name="sq_b", tag="sq_b", align_bytes=64)
+                nc.scalar.activation(sq_a[:], pair[:, 0:HALF], ACT.Square)
+                nc.scalar.activation(sq_b[:], pair[:, HALF:S], ACT.Square)
+                nc.vector.scalar_tensor_tensor(total[:], sq_a[:], 4.0, sq_b[:], ALU.mult, ALU.add)
+                y_win = keep.tile([P, S], F32, name="y_win%d" % t, tag="sq_a", align_bytes=64)
+                nc.vector.tensor_tensor(y_win[:].indirect(n3_t[:]), pair[:, 0:HALF], pair[:, HALF:S], ALU.add)
             y_wins.append(y_win)
-            nc.vector.tensor_tensor(y_win[:].indirect(n3_t[:]), pair[:, 0:HALF], pair[:, HALF:S], ALU.add)
-            nc.scalar.activation(root[:], total[:], ACT.Sqrt, bias=quarter[:])
-            nc.vector.tensor_copy(y_win[:].indirect(n2_t[:]), root[:])
-            nc.sync.dma_start(out_rows[:, t, :], y_win[:])
-        for t in range(3):
+            if t > 0:
+                finish(t - 1, "h2_win%d" % t if t < 3 else "sq_b")
+        finish(3, "root3")
+        for t in range(2):
             nc.scalar.copy(y_rows[:, t, :], y_wins[t][:])
 
         y_grouped = keep.tile([P, S, 4], BF16, name="y_grouped", align_bytes=64)
         y_codes = keep.tile([P, S], U32, name="y_codes", align_bytes=64)
         y_scales = keep.tile([P, S], U8, name="y_scales", align_bytes=64)
-        nc.scalar.copy(y_grouped[:, 0:HALF, 0:2], y_rows[:, 0:2, 0:HALF].rearrange("p t c -> p c t"))
-        nc.scalar.copy(y_grouped[:, HALF:S, 0:3], y_rows[:, 0:3, HALF:S].rearrange("p t c -> p c t"))
+        nc.scalar.copy(y_grouped[:, :, 0:2], y_rows[:, 0:2, :].rearrange("p t c -> p c t"))
+        nc.scalar.copy(y_rows[:, 2, 0:HALF], y_wins[2][:, 0:HALF])
+        nc.scalar.copy(y_grouped[:, HALF:S, 2], y_wins[2][:, HALF:S])
         nc.vector.tensor_copy(y_rows[:, 3, 0:HALF], y_wins[3][:, 0:HALF])
         nc.scalar.copy(y_grouped[:, HALF:S, 3], y_wins[3][:, HALF:S])
         nc.vector.tensor_copy(y_grouped[:, 0:HALF, 2:4], y_rows[:, 2:4, 0:HALF].rearrange("p t c -> p c t"))

@@ -14,9 +14,16 @@ ACT = mybir.ActivationFunctionType
 ALU = mybir.AluOpType
 
 P = 128
-T = 2048
+PACK = 4
+TABLE = 2048
 S = 512
-HALF = 256
+HALF = S // 2
+PER_COLUMN = 16
+H_FACTOR = 0.0625
+STRETCHES = [(0, 256), (256, 384), (384, 512)]
+LAST = len(STRETCHES) - 1
+LATE = STRETCHES[LAST][0]
+FIRST_TILES = 2
 FLOPS = 2 * 2 * 512 * 512 * 512
 
 
@@ -29,206 +36,217 @@ def tile_picked_pqlaygatepolar_none_po_kernel(
         keep = ctx.enter_context(tc.tile_pool(name="keep", bufs=1))
         psum = ctx.enter_context(tc.psum_pool(name="psum", bufs=1))
 
-        k1_t = lists.tile([P, S // 16], U16, name="k1_t")
-        offs_t = lists.tile([P, S // 16], U16, name="offs_t")
-        n1_t = lists.tile([P, S // 16], U16, name="n1_t")
-        n2_t = lists.tile([P, HALF // 16], U16, name="n2_t")
-        n3_t = lists.tile([P, HALF // 16], U16, name="n3_t")
+        k1_list = lists.tile([P, S // PER_COLUMN], U16, name="k1_list")
+        offs_list = lists.tile([P, S // PER_COLUMN], U16, name="offs_list")
+        n1_list = lists.tile([P, S // PER_COLUMN], U16, name="n1_list")
+        n2_list = lists.tile([P, HALF // PER_COLUMN], U16, name="n2_list")
+        n3_list = lists.tile([P, HALF // PER_COLUMN], U16, name="n3_list")
 
-        ds_win = keep.tile([P, T], U8, name="ds_win", tag="ds_win", align_bytes=64)
-        xs_win = keep.tile([P, T], U8, name="xs_win", tag="xs_win", align_bytes=64)
-        dw_win = keep.tile([P, T], I32, name="dw_win", tag="dw_win", align_bytes=64)
-        xw_win = keep.tile([P, T], I32, name="xw_win", align_bytes=64)
-        gain = keep.tile([P, 4], F32, name="gain")
-        gain16 = keep.tile([P, 4], F32, name="gain16")
+        d_scale_win = keep.tile([P, TABLE], U8, name="d_scale_win", align_bytes=64)
+        x_scale_win = keep.tile([P, TABLE], U8, name="x_scale_win", align_bytes=64)
+        d_word_win = keep.tile([P, TABLE], I32, name="d_word_win", tag="d_words", align_bytes=64)
+        x_word_win = keep.tile([P, TABLE], I32, name="x_word_win", align_bytes=64)
+        gain = keep.tile([P, PACK], F32, name="gain")
+        scaled_gain = keep.tile([P, PACK], F32, name="scaled_gain")
         quarter = keep.tile([P, 1], F32, name="quarter")
 
-        nc.gpsimd.memset(ds_win[:].bitcast(I32), 0)
-        nc.vector.memset(xs_win[:].bitcast(I32), 0)
-        nc.sync.dma_start(k1_t[:], k1)
-        nc.sync.dma_start(ds_win[0:P:8, :].bitcast(I32), d_scales[0].bitcast(I32))
-        nc.sync.dma_start(offs_t[:], offs)
-        nc.sync.dma_start(xs_win[0:P:8, :].bitcast(I32), x_scales[0].bitcast(I32))
-        nc.sync.dma_start(n1_t[:], n1)
-        nc.sync.dma_start(dw_win[:], d_words[0].rearrange("p n t -> p (n t)").bitcast(I32))
-        nc.sync.dma_start(xw_win[:], x_words[0].rearrange("p n t -> p (n t)").bitcast(I32))
-        nc.sync.dma_start(n2_t[:], n2)
-        nc.sync.dma_start(n3_t[:], n3)
-        nc.gpsimd.dma_start(gain[:], gn.rearrange("(p t) o -> p (t o)", t=4))
+        nc.gpsimd.memset(d_scale_win[:].bitcast(I32), 0)
+        nc.vector.memset(x_scale_win[:].bitcast(I32), 0)
+        nc.sync.dma_start(k1_list[:], k1)
+        nc.sync.dma_start(d_scale_win[0:P:8, :].bitcast(I32), d_scales[0].bitcast(I32))
+        nc.sync.dma_start(offs_list[:], offs)
+        nc.sync.dma_start(x_scale_win[0:P:8, :].bitcast(I32), x_scales[0].bitcast(I32))
+        nc.sync.dma_start(n1_list[:], n1)
+        nc.sync.dma_start(d_word_win[:], d_words[0].rearrange("p n t -> p (n t)").bitcast(I32))
+        nc.sync.dma_start(x_word_win[:], x_words[0].rearrange("p n t -> p (n t)").bitcast(I32))
+        nc.sync.dma_start(n2_list[:], n2)
+        nc.sync.dma_start(n3_list[:], n3)
+        nc.gpsimd.dma_start(gain[:], gn.rearrange("(p t) o -> p (t o)", t=PACK))
         nc.gpsimd.memset(quarter[:], 0.25)
-        nc.gpsimd.tensor_scalar(gain16[:], gain[:], 0.0625, 0.0, ALU.mult, ALU.add)
+        nc.gpsimd.tensor_scalar(scaled_gain[:], gain[:], H_FACTOR, 0.0, ALU.mult, ALU.add)
 
-        ds_got = keep.tile([P, S], U8, name="ds_got", align_bytes=64)
-        xs_got = keep.tile([P, S], U8, name="xs_got", tag="got", align_bytes=64)
-        planes = keep.tile([P, 2 * S], U8, name="planes", align_bytes=64)
-        nc.vector.tensor_copy(ds_got[:], ds_win[:].indirect(k1_t[:]))
-        nc.vector.tensor_copy(xs_got[:], xs_win[:].indirect(offs_t[:]))
+        d_scale_picked = keep.tile([P, S], U8, name="d_scale_picked", tag="picked", align_bytes=64)
+        x_scale_picked = keep.tile([P, S], U8, name="x_scale_picked", align_bytes=64)
+        scales1 = keep.tile([P, 2 * S], U8, name="scales1", align_bytes=64)
+        nc.vector.tensor_copy(d_scale_picked[:], d_scale_win[:].indirect(k1_list[:]))
+        nc.vector.tensor_copy(x_scale_picked[:], x_scale_win[:].indirect(offs_list[:]))
         nc.vector.tensor_copy(
-            planes[:, 0:S].rearrange("p (t m) -> p t m", t=4), ds_got[:].rearrange("p (m t) -> p t m", t=4)
+            scales1[:, 0:S].rearrange("p (t m) -> p t m", t=PACK),
+            d_scale_picked[:].rearrange("p (m t) -> p t m", t=PACK),
         )
-        nc.vector.tensor_copy(planes[:, S : 2 * S].bitcast(I32), xs_got[:].bitcast(I32))
-        for c in range(1, 4):
-            nc.scalar.dma_start(planes[c:P:32, :].bitcast(I32), planes[8 * c : P : 32, :].bitcast(I32))
+        nc.vector.tensor_copy(scales1[:, S : 2 * S].bitcast(I32), x_scale_picked[:].bitcast(I32))
+        for c in range(1, PACK):
+            nc.scalar.dma_start(scales1[c:P:32, :].bitcast(I32), scales1[8 * c : P : 32, :].bitcast(I32))
 
-        dw_got = keep.tile([P, S], U32, name="dw_got", tag="got", align_bytes=64)
-        dw_dealt = keep.tile([P, S], U32, name="dw_dealt", align_bytes=64)
-        nc.vector.tensor_copy(dw_got[:], dw_win[:].bitcast(U32).indirect(k1_t[:]))
+        d_word_picked = keep.tile([P, S], U32, name="d_word_picked", tag="picked", align_bytes=64)
+        d_word_dealt = keep.tile([P, S], U32, name="d_word_dealt", align_bytes=64)
+        nc.vector.tensor_copy(d_word_picked[:], d_word_win[:].bitcast(U32).indirect(k1_list[:]))
         nc.vector.tensor_copy(
-            dw_dealt[:].rearrange("p (t m) -> p t m", t=4), dw_got[:].rearrange("p (m t) -> p t m", t=4)
+            d_word_dealt[:].rearrange("p (t m) -> p m t", t=PACK),
+            d_word_picked[:].rearrange("p (m t) -> p m t", t=PACK),
         )
 
-        xw_got = [keep.tile([P, HALF], U32, name="xw_got%d" % u, align_bytes=64) for u in range(2)]
-        h_win = [keep.tile([P, S], F32, name="h_win%d" % t, align_bytes=64) for t in range(4)]
-        acc1 = [psum.tile([P, S], F32, name="acc1_%d" % t, tag="bank%d" % t) for t in range(4)]
+        x_word_picked = [keep.tile([P, HALF], U32, name="x_word_picked%d" % u, align_bytes=64) for u in range(2)]
+        gate_win = [keep.tile([P, S], F32, name="gate_win%d" % t, align_bytes=64) for t in range(PACK)]
+        sums1 = {}
+        whole_sums1 = {}
+        for t in range(PACK):
+            if t < FIRST_TILES:
+                for u in range(2):
+                    bank = psum.tile([P, HALF], F32, name="sums1_%d_%d" % (t, u), tag="bank%d" % (2 * t + u))
+                    sums1[t, u] = bank[:]
+            else:
+                bank = psum.tile([P, S], F32, name="sums1_%d" % t, tag="bank%d" % (FIRST_TILES + t))
+                whole_sums1[t] = bank[:]
+                for u in range(2):
+                    sums1[t, u] = bank[:, HALF * u : HALF * (u + 1)]
         for u in range(2):
-            nc.vector.tensor_copy(xw_got[u][:], xw_win[:].bitcast(U32).indirect(offs_t[:, 16 * u : 16 * (u + 1)]))
-        for t, u in [(0, 0), (1, 0), (0, 1), (1, 1), (2, 0), (2, 1), (3, 0), (3, 1)]:
+            entries = offs_list[:, HALF * u // PER_COLUMN : HALF * (u + 1) // PER_COLUMN]
+            nc.vector.tensor_copy(x_word_picked[u][:], x_word_win[:].bitcast(U32).indirect(entries))
+        order = [(t, u) for u in range(2) for t in range(FIRST_TILES)]
+        order = order + [(t, u) for t in range(FIRST_TILES, PACK) for u in range(2)]
+        for t, u in order:
             nc.tensor.matmul_mx(
-                out=acc1[t][:, HALF * u : HALF * (u + 1)],
-                lhsT=dw_dealt[:, P * t : P * (t + 1)].bitcast(FP8X4),
-                lhsT_scale=planes[:, P * t : P * (t + 1)],
-                rhs=xw_got[u][:].bitcast(FP8X4),
-                rhs_scale=planes[:, S + HALF * u : S + HALF * (u + 1)],
+                out=sums1[t, u],
+                lhsT=d_word_dealt[:, P * t : P * (t + 1)].bitcast(FP8X4),
+                lhsT_scale=scales1[:, P * t : P * (t + 1)],
+                rhs=x_word_picked[u][:].bitcast(FP8X4),
+                rhs_scale=scales1[:, S + HALF * u : S + HALF * (u + 1)],
                 start=True,
                 stop=True,
             )
-            if u == 1 and t == 0:
-                nc.scalar.activation(h_win[t][:], acc1[t][:], ACT.Sigmoid, scale=0.0625)
-            elif u == 1 and t == 1:
-                nc.vector.tensor_copy(h_win[t][:], acc1[t][:])
+            if t < FIRST_TILES:
+                nc.scalar.activation(gate_win[t][:, HALF * u : HALF * (u + 1)], sums1[t, u], ACT.Sigmoid, scale=H_FACTOR)
             elif u == 1:
-                nc.scalar.copy(h_win[t][:], acc1[t][:])
+                nc.scalar.copy(gate_win[t][:], whole_sums1[t])
 
-        ww_raw = keep.tile([P, 2 * S], U8, name="ww_raw", tag="dw_win", align_bytes=64)
-        ws_raw = keep.tile([P, S], U8, name="ws_raw", tag="xs_win", align_bytes=64)
-        ww_dealt = keep.tile([P, 2 * S], U8, name="ww_dealt", align_bytes=64)
-        ws_dealt = keep.tile([P, S], U8, name="ws_dealt", align_bytes=64)
-        nc.gpsimd.memset(ws_raw[:].bitcast(I32), 0)
-        nc.sync.dma_start(ww_raw[:].bitcast(I32), w1_words[0].bitcast(I32))
+        w_word_raw = keep.tile([P, 2 * S], U8, name="w_word_raw", tag="d_words", align_bytes=64)
+        w_scale_raw = keep.tile([P, S], U8, name="w_scale_raw", tag="picked", align_bytes=64)
+        w_word_dealt = keep.tile([P, 2 * S], U8, name="w_word_dealt", align_bytes=64)
+        w_scale_dealt = keep.tile([P, S], U8, name="w_scale_dealt", align_bytes=64)
+        nc.gpsimd.memset(w_scale_raw[:].bitcast(I32), 0)
+        nc.sync.dma_start(w_word_raw[:].bitcast(I32), w1_words[0].bitcast(I32))
         for q in range(4):
             nc.sync.dma_start(
-                ws_raw[32 * q : 32 * q + 4, :].bitcast(I32), w1_scales[0, 4 * q : 4 * q + 4, :].bitcast(I32)
+                w_scale_raw[32 * q : 32 * q + 4, :].bitcast(I32), w1_scales[0, 4 * q : 4 * q + 4, :].bitcast(I32)
             )
         nc.gpsimd.tensor_copy(
-            ww_dealt[:].rearrange("p (t m b) -> p t m b", t=4, b=2),
-            ww_raw[:].rearrange("p (m t b) -> p t m b", t=4, b=2),
+            w_word_dealt[:].rearrange("p (t m b) -> p t m b", t=PACK, b=2),
+            w_word_raw[:].rearrange("p (m t b) -> p t m b", t=PACK, b=2),
         )
         nc.gpsimd.tensor_copy(
-            ws_dealt[:].rearrange("p (t m) -> p t m", t=4), ws_raw[:].rearrange("p (m t) -> p t m", t=4)
+            w_scale_dealt[:].rearrange("p (t m) -> p t m", t=PACK),
+            w_scale_raw[:].rearrange("p (m t) -> p t m", t=PACK),
         )
 
-        h2_win = [keep.tile([P, S], F32, name="h2_win%d" % t, tag="h2_win%d" % t, align_bytes=64) for t in range(3)]
-        chunks = [(0, 256), (256, 384), (384, 512)]
-        early = {}
-        late = {}
-        for c, (lo, hi) in enumerate(chunks):
-            n = hi - lo
-            z_rows = keep.tile([P, 4, n], BF16, name="z_rows%d" % c, align_bytes=64)
-            for t in range(4):
+        z_codes = keep.tile([P, S], U32, name="z_codes", align_bytes=64)
+        z_scales = keep.tile([P, S], U8, name="z_scales", align_bytes=64)
+        early_sums2 = [psum.tile([P, LATE], F32, name="early_sums2_%d" % t, tag="bank%d" % (6 + t)) for t in range(2)]
+        late_sums2 = {}
+        h2_win = [keep.tile([P, S], F32, name="h2_win0", tag="even_tiles", align_bytes=64)]
+
+        def second_product(t, lo, hi, sums):
+            nc.tensor.matmul_mx(
+                out=sums,
+                lhsT=w_word_dealt[:, 2 * P * t : 2 * P * (t + 1)].bitcast(FP4X4),
+                lhsT_scale=w_scale_dealt[:, P * t : P * (t + 1)],
+                rhs=z_codes[:, lo:hi].bitcast(FP8X4),
+                rhs_scale=z_scales[:, lo:hi],
+                start=True,
+                stop=True,
+            )
+
+        for c, (lo, hi) in enumerate(STRETCHES):
+            width = hi - lo
+            u = lo // HALF
+            z_rows = keep.tile([P, PACK, width], BF16, name="z_rows%d" % c, align_bytes=64)
+            for t in range(PACK):
                 tag = "gate%d" % t if t > 0 else "gate0_%d" % c
-                gate = keep.tile([P, n], F32, name="gate%d_%d" % (t, c), tag=tag, align_bytes=64)
-                picked = h_win[t][:].indirect(n1_t[:, lo // 16 : hi // 16])
-                if t == 0:
+                gate = keep.tile([P, width], F32, name="gate%d_%d" % (t, c), tag=tag, align_bytes=64)
+                picked = gate_win[t][:].indirect(n1_list[:, lo // PER_COLUMN : hi // PER_COLUMN])
+                if t == 0 or (t == 1 and c == 0):
                     nc.vector.tensor_copy(gate[:], picked)
+                elif t < FIRST_TILES:
+                    nc.scalar.activation(gate[:], picked, ACT.Copy)
                 else:
-                    nc.scalar.activation(gate[:], picked, ACT.Sigmoid, scale=0.0625)
+                    nc.scalar.activation(gate[:], picked, ACT.Sigmoid, scale=H_FACTOR)
                 nc.vector.scalar_tensor_tensor(
                     z_rows[:, t, :],
-                    acc1[t][:, lo:hi],
-                    gain16[:, t : t + 1],
+                    sums1[t, u][:, lo - HALF * u : hi - HALF * u],
+                    scaled_gain[:, t : t + 1],
                     gate[:],
                     ALU.mult,
                     ALU.mult,
                 )
-            if c == 2:
+            if c == LAST:
                 warm = keep.tile([P, 1], F32, name="warm")
                 nc.scalar.activation(warm[:], gate[:, 0:1], ACT.Sqrt, bias=quarter[:])
-            z_grouped = keep.tile([P, n, 4], BF16, name="z_grouped%d" % c, align_bytes=64)
-            z_codes = keep.tile([P, n], U32, name="z_codes%d" % c, align_bytes=64)
-            z_scales = keep.tile([P, n], U8, name="z_scales%d" % c, align_bytes=64)
+            tag = "odd_tiles" if c == LAST else "z_grouped%d" % c
+            z_grouped = keep.tile([P, width, PACK], BF16, name="z_grouped%d" % c, tag=tag, align_bytes=64)
             nc.vector.tensor_copy(
                 z_grouped[:].rearrange("p (c i) t -> p c t i", i=4),
                 z_rows[:].rearrange("p t (c i) -> p c t i", i=4),
             )
             nc.vector.quantize_mx(
-                out=z_codes[:].bitcast(FP8X4), scales=z_scales[:], in_=z_grouped[:].rearrange("p c t -> p (c t)")
+                out=z_codes[:, lo:hi].bitcast(FP8X4),
+                scales=z_scales[:, lo:hi],
+                in_=z_grouped[:].rearrange("p c t -> p (c t)"),
             )
-            for t in range(4):
-                if c == 0:
-                    early[t] = psum.tile([P, S], F32, name="early%d" % t, tag="bank%d" % (4 + t))
-                if c == 2 and t < 3:
-                    late[t] = psum.tile([P, n], F32, name="late%d" % t, tag="bank%d" % t)
-                nc.tensor.matmul_mx(
-                    out=early[t][:, lo:hi] if c < 2 or t == 3 else late[t][:],
-                    lhsT=ww_dealt[:, 2 * P * t : 2 * P * (t + 1)].bitcast(FP4X4),
-                    lhsT_scale=ws_dealt[:, P * t : P * (t + 1)],
-                    rhs=z_codes[:].bitcast(FP8X4),
-                    rhs_scale=z_scales[:],
-                    start=True,
-                    stop=True,
-                )
-                if c == 1 and t < 2:
-                    nc.scalar.copy(h2_win[t][:, 0:384], early[t][:, 0:384])
+            for t in range(FIRST_TILES):
+                if c == LAST:
+                    late_sums2[t] = psum.tile([P, width], F32, name="late_sums2_%d" % t, tag="bank%d" % (2 * t))
+                second_product(t, lo, hi, late_sums2[t][:] if c == LAST else early_sums2[t][:, lo:hi])
+            if hi == LATE:
+                nc.scalar.copy(h2_win[0][:, 0:LATE], early_sums2[0][:])
+        for t in range(FIRST_TILES, PACK):
+            late_sums2[t] = psum.tile([P, S], F32, name="late_sums2_%d" % t, tag="bank%d" % (2 * t - 3))
+            second_product(t, 0, S, late_sums2[t][:])
 
-        out_rows = out_0.rearrange("(p t) c -> p t c", t=4)
-        y_rows = keep.tile([P, 4, S], BF16, name="y_rows", align_bytes=64)
-        y_wins = []
+        out_rows = out_0.rearrange("(p t) c -> p t c", t=PACK)
+        h2_win.append(keep.tile([P, S], F32, name="h2_win1", tag="odd_tiles", align_bytes=64))
+        nc.vector.tensor_copy(h2_win[1][:, 0:LATE], early_sums2[1][:])
+        for t in range(FIRST_TILES):
+            nc.vector.tensor_copy(h2_win[t][:, LATE:S], late_sums2[t][:])
+        pairs = []
+        y_win = []
+        for t in range(PACK):
+            if t >= FIRST_TILES:
+                tag = "even_tiles" if t % 2 == 0 else "odd_tiles"
+                h2_win.append(keep.tile([P, S], F32, name="h2_win%d" % t, tag=tag, align_bytes=64))
+                nc.scalar.copy(h2_win[t][:], late_sums2[t][:])
+            pairs.append(keep.tile([P, S], F32, name="pair%d" % t, align_bytes=64))
+            y_win.append(keep.tile([P, S], F32, name="y_win%d" % t, align_bytes=64))
+            nc.scalar.activation(pairs[t][:, 0:HALF], h2_win[t][:].indirect(n2_list[:]), ACT.Copy, scale=-0.5)
+            if t < FIRST_TILES:
+                nc.vector.tensor_copy(pairs[t][:, HALF:S], h2_win[t][:].indirect(n3_list[:]))
+            else:
+                nc.scalar.activation(pairs[t][:, HALF:S], h2_win[t][:].indirect(n3_list[:]), ACT.Copy)
+            nc.vector.tensor_tensor(y_win[t][:].indirect(n3_list[:]), pairs[t][:, 0:HALF], pairs[t][:, HALF:S], ALU.add)
         totals = []
-
-        def finish(t, tag):
-            root = keep.tile([P, HALF], F32, name="root%d" % t, tag=tag, align_bytes=64)
+        for t in range(PACK):
+            squares = keep.tile([P, S], F32, name="squares%d" % t, align_bytes=64)
+            totals.append(keep.tile([P, HALF], F32, name="total%d" % t, tag="total%d" % t, align_bytes=64))
+            nc.scalar.activation(squares[:], pairs[t][:], ACT.Square)
+            nc.vector.scalar_tensor_tensor(
+                totals[t][:], squares[:, 0:HALF], 4.0, squares[:, HALF:S], ALU.mult, ALU.add
+            )
+        for t in range(PACK):
+            root = keep.tile([P, HALF], F32, name="root%d" % t, align_bytes=64)
             nc.scalar.activation(root[:], totals[t][:], ACT.Sqrt, bias=quarter[:])
-            nc.vector.tensor_copy(y_wins[t][:].indirect(n2_t[:]), root[:])
-            nc.sync.dma_start(out_rows[:, t, :], y_wins[t][:])
+            nc.vector.tensor_copy(y_win[t][:].indirect(n2_list[:]), root[:])
+            nc.sync.dma_start(out_rows[:, t, :], y_win[t][:])
 
-        nc.vector.tensor_copy(h2_win[2][:, 0:384], early[2][:, 0:384])
-        for t in range(2):
-            nc.vector.tensor_copy(h2_win[t][:, 384:S], late[t][:])
-        for t in range(4):
-            if t == 3:
-                h2_win.append(keep.tile([P, S], F32, name="h2_win3", tag="h2_win0", align_bytes=64))
-                nc.scalar.copy(h2_win[3][:], early[3][:])
-            pair = keep.tile([P, S], F32, name="pair%d" % t, align_bytes=64)
-            total = keep.tile([P, HALF], F32, name="total%d" % t, align_bytes=64)
-            totals.append(total)
-            nc.scalar.activation(pair[:, 0:HALF], h2_win[t][:].indirect(n2_t[:]), ACT.Copy, scale=-0.5)
-            if t == 0:
-                nc.vector.tensor_copy(pair[:, HALF:S], h2_win[t][:].indirect(n3_t[:]))
-                nc.vector.tensor_copy(h2_win[2][:, 384:S], late[2][:])
-            else:
-                nc.scalar.activation(pair[:, HALF:S], h2_win[t][:].indirect(n3_t[:]), ACT.Copy)
-            if t < 3:
-                squares = keep.tile([P, S], F32, name="squares%d" % t, align_bytes=64)
-                nc.scalar.activation(squares[:], pair[:], ACT.Square)
-                y_win = keep.tile([P, S], F32, name="y_win%d" % t, align_bytes=64)
-                nc.vector.tensor_tensor(y_win[:].indirect(n3_t[:]), pair[:, 0:HALF], pair[:, HALF:S], ALU.add)
-                nc.vector.scalar_tensor_tensor(
-                    total[:], squares[:, 0:HALF], 4.0, squares[:, HALF:S], ALU.mult, ALU.add
-                )
-            else:
-                sq_a = keep.tile([P, HALF], F32, name="sq_a", tag="sq_a", align_bytes=64)
-                sq_b = keep.tile([P, HALF], F32, name="sq_b", tag="sq_b", align_bytes=64)
-                nc.scalar.activation(sq_a[:], pair[:, 0:HALF], ACT.Square)
-                nc.scalar.activation(sq_b[:], pair[:, HALF:S], ACT.Square)
-                nc.vector.scalar_tensor_tensor(total[:], sq_a[:], 4.0, sq_b[:], ALU.mult, ALU.add)
-                y_win = keep.tile([P, S], F32, name="y_win%d" % t, tag="sq_a", align_bytes=64)
-                nc.vector.tensor_tensor(y_win[:].indirect(n3_t[:]), pair[:, 0:HALF], pair[:, HALF:S], ALU.add)
-            y_wins.append(y_win)
-            if t > 0:
-                finish(t - 1, "h2_win%d" % t if t < 3 else "sq_b")
-        finish(3, "root3")
-        for t in range(2):
-            nc.scalar.copy(y_rows[:, t, :], y_wins[t][:])
-
-        y_grouped = keep.tile([P, S, 4], BF16, name="y_grouped", align_bytes=64)
+        y_grouped = keep.tile([P, S, PACK], BF16, name="y_grouped", tag="total3", align_bytes=64)
+        y_left = keep.tile([P, 2, HALF], BF16, name="y_left", tag="total2", align_bytes=64)
         y_codes = keep.tile([P, S], U32, name="y_codes", align_bytes=64)
         y_scales = keep.tile([P, S], U8, name="y_scales", align_bytes=64)
-        nc.scalar.copy(y_grouped[:, :, 0:2], y_rows[:, 0:2, :].rearrange("p t c -> p c t"))
-        nc.scalar.copy(y_rows[:, 2, 0:HALF], y_wins[2][:, 0:HALF])
-        nc.scalar.copy(y_grouped[:, HALF:S, 2], y_wins[2][:, HALF:S])
-        nc.vector.tensor_copy(y_rows[:, 3, 0:HALF], y_wins[3][:, 0:HALF])
-        nc.scalar.copy(y_grouped[:, HALF:S, 3], y_wins[3][:, HALF:S])
-        nc.vector.tensor_copy(y_grouped[:, 0:HALF, 2:4], y_rows[:, 2:4, 0:HALF].rearrange("p t c -> p c t"))
+        for t in range(2):
+            nc.scalar.copy(y_grouped[:, :, t], y_win[t][:])
+        nc.scalar.copy(y_left[:, 0, :], y_win[2][:, 0:HALF])
+        nc.scalar.copy(y_grouped[:, HALF:S, 2], y_win[2][:, HALF:S])
+        nc.vector.tensor_copy(y_left[:, 1, :], y_win[3][:, 0:HALF])
+        nc.scalar.copy(y_grouped[:, HALF:S, 3], y_win[3][:, HALF:S])
+        nc.vector.tensor_copy(y_grouped[:, 0:HALF, 2:4], y_left[:].rearrange("p t c -> p c t"))
         words_out = out_1[0].rearrange("p n t -> p (n t)").bitcast(I32)
         for u in range(2):
             cols = slice(HALF * u, HALF * (u + 1))
@@ -239,5 +257,5 @@ def tile_picked_pqlaygatepolar_none_po_kernel(
             )
             nc.sync.dma_start(words_out[:, cols], y_codes[:, cols].bitcast(I32))
         for q in range(4):
-            eng = nc.scalar if q % 2 == 0 else nc.sync
-            eng.dma_start(out_2[0, 4 * q : 4 * q + 4, :].bitcast(I32), y_scales[32 * q : 32 * q + 4, :].bitcast(I32))
+            queue = nc.scalar if q % 2 == 0 else nc.sync
+            queue.dma_start(out_2[0, 4 * q : 4 * q + 4, :].bitcast(I32), y_scales[32 * q : 32 * q + 4, :].bitcast(I32))

from contextlib import ExitStack

import concourse.mybir as mybir

F32 = mybir.dt.float32
BF16 = mybir.dt.bfloat16
I32 = mybir.dt.int32
U32 = mybir.dt.uint32
U16 = mybir.dt.uint16
U8 = mybir.dt.uint8
FP8X4 = mybir.dt.float8_e4m3fn_x4
FP4X4 = mybir.dt.float4_e2m1fn_x4
ACT = mybir.ActivationFunctionType
ALU = mybir.AluOpType

P = 128
PACK = 4
TABLE = 2048
S = 512
HALF = S // 2
PER_COLUMN = 16
H_FACTOR = 0.0625
STRETCHES = [(0, 256), (256, 384), (384, 512)]
LAST = len(STRETCHES) - 1
LATE = STRETCHES[LAST][0]
FIRST_TILES = 2
FLOPS = 2 * 2 * 512 * 512 * 512


def tile_picked_pqlaygatepolar_none_po_kernel(
    tc, x_words, x_scales, d_words, d_scales, gn, w1_words, w1_scales, offs, k1, n1, n2, n3, out_0, out_1, out_2
):
    nc = tc.nc
    with ExitStack() as ctx:
        lists = ctx.enter_context(tc.tile_pool(name="lists", bufs=1))
        keep = ctx.enter_context(tc.tile_pool(name="keep", bufs=1))
        psum = ctx.enter_context(tc.psum_pool(name="psum", bufs=1))

        k1_list = lists.tile([P, S // PER_COLUMN], U16, name="k1_list")
        offs_list = lists.tile([P, S // PER_COLUMN], U16, name="offs_list")
        n1_list = lists.tile([P, S // PER_COLUMN], U16, name="n1_list")
        n2_list = lists.tile([P, HALF // PER_COLUMN], U16, name="n2_list")
        n3_list = lists.tile([P, HALF // PER_COLUMN], U16, name="n3_list")

        d_scale_win = keep.tile([P, TABLE], U8, name="d_scale_win", align_bytes=64)
        x_scale_win = keep.tile([P, TABLE], U8, name="x_scale_win", align_bytes=64)
        d_word_win = keep.tile([P, TABLE], I32, name="d_word_win", tag="d_words", align_bytes=64)
        x_word_win = keep.tile([P, TABLE], I32, name="x_word_win", align_bytes=64)
        gain = keep.tile([P, PACK], F32, name="gain")
        scaled_gain = keep.tile([P, PACK], F32, name="scaled_gain")
        quarter = keep.tile([P, 1], F32, name="quarter")

        nc.gpsimd.memset(d_scale_win[:].bitcast(I32), 0)
        nc.vector.memset(x_scale_win[:].bitcast(I32), 0)
        nc.sync.dma_start(k1_list[:], k1)
        nc.sync.dma_start(d_scale_win[0:P:8, :].bitcast(I32), d_scales[0].bitcast(I32))
        nc.sync.dma_start(offs_list[:], offs)
        nc.sync.dma_start(x_scale_win[0:P:8, :].bitcast(I32), x_scales[0].bitcast(I32))
        nc.sync.dma_start(n1_list[:], n1)
        nc.sync.dma_start(d_word_win[:], d_words[0].rearrange("p n t -> p (n t)").bitcast(I32))
        nc.sync.dma_start(x_word_win[:], x_words[0].rearrange("p n t -> p (n t)").bitcast(I32))
        nc.sync.dma_start(n2_list[:], n2)
        nc.sync.dma_start(n3_list[:], n3)
        nc.gpsimd.dma_start(gain[:], gn.rearrange("(p t) o -> p (t o)", t=PACK))
        nc.gpsimd.memset(quarter[:], 0.25)
        nc.gpsimd.tensor_scalar(scaled_gain[:], gain[:], H_FACTOR, 0.0, ALU.mult, ALU.add)

        d_scale_picked = keep.tile([P, S], U8, name="d_scale_picked", tag="picked", align_bytes=64)
        x_scale_picked = keep.tile([P, S], U8, name="x_scale_picked", align_bytes=64)
        scales1 = keep.tile([P, 2 * S], U8, name="scales1", align_bytes=64)
        nc.vector.tensor_copy(d_scale_picked[:], d_scale_win[:].indirect(k1_list[:]))
        nc.vector.tensor_copy(x_scale_picked[:], x_scale_win[:].indirect(offs_list[:]))
        nc.vector.tensor_copy(
            scales1[:, 0:S].rearrange("p (t m) -> p t m", t=PACK),
            d_scale_picked[:].rearrange("p (m t) -> p t m", t=PACK),
        )
        nc.vector.tensor_copy(scales1[:, S : 2 * S].bitcast(I32), x_scale_picked[:].bitcast(I32))
        for c in range(1, PACK):
            nc.scalar.dma_start(scales1[c:P:32, :].bitcast(I32), scales1[8 * c : P : 32, :].bitcast(I32))

        d_word_picked = keep.tile([P, S], U32, name="d_word_picked", tag="picked", align_bytes=64)
        d_word_dealt = keep.tile([P, S], U32, name="d_word_dealt", align_bytes=64)
        nc.vector.tensor_copy(d_word_picked[:], d_word_win[:].bitcast(U32).indirect(k1_list[:]))
        nc.vector.tensor_copy(
            d_word_dealt[:].rearrange("p (t m) -> p m t", t=PACK),
            d_word_picked[:].rearrange("p (m t) -> p m t", t=PACK),
        )

        x_word_picked = [keep.tile([P, HALF], U32, name="x_word_picked%d" % u, align_bytes=64) for u in range(2)]
        gate_win = [keep.tile([P, S], F32, name="gate_win%d" % t, align_bytes=64) for t in range(PACK)]
        sums1 = {}
        whole_sums1 = {}
        for t in range(PACK):
            if t < FIRST_TILES:
                for u in range(2):
                    bank = psum.tile([P, HALF], F32, name="sums1_%d_%d" % (t, u), tag="bank%d" % (2 * t + u))
                    sums1[t, u] = bank[:]
            else:
                bank = psum.tile([P, S], F32, name="sums1_%d" % t, tag="bank%d" % (FIRST_TILES + t))
                whole_sums1[t] = bank[:]
                for u in range(2):
                    sums1[t, u] = bank[:, HALF * u : HALF * (u + 1)]
        for u in range(2):
            entries = offs_list[:, HALF * u // PER_COLUMN : HALF * (u + 1) // PER_COLUMN]
            nc.vector.tensor_copy(x_word_picked[u][:], x_word_win[:].bitcast(U32).indirect(entries))
        order = [(t, u) for u in range(2) for t in range(FIRST_TILES)]
        order = order + [(t, u) for t in range(FIRST_TILES, PACK) for u in range(2)]
        for t, u in order:
            nc.tensor.matmul_mx(
                out=sums1[t, u],
                lhsT=d_word_dealt[:, P * t : P * (t + 1)].bitcast(FP8X4),
                lhsT_scale=scales1[:, P * t : P * (t + 1)],
                rhs=x_word_picked[u][:].bitcast(FP8X4),
                rhs_scale=scales1[:, S + HALF * u : S + HALF * (u + 1)],
                start=True,
                stop=True,
            )
            if t < FIRST_TILES:
                nc.scalar.activation(gate_win[t][:, HALF * u : HALF * (u + 1)], sums1[t, u], ACT.Sigmoid, scale=H_FACTOR)
            elif u == 1:
                nc.scalar.copy(gate_win[t][:], whole_sums1[t])

        w_word_raw = keep.tile([P, 2 * S], U8, name="w_word_raw", tag="d_words", align_bytes=64)
        w_scale_raw = keep.tile([P, S], U8, name="w_scale_raw", tag="picked", align_bytes=64)
        w_word_dealt = keep.tile([P, 2 * S], U8, name="w_word_dealt", align_bytes=64)
        w_scale_dealt = keep.tile([P, S], U8, name="w_scale_dealt", align_bytes=64)
        nc.gpsimd.memset(w_scale_raw[:].bitcast(I32), 0)
        nc.sync.dma_start(w_word_raw[:].bitcast(I32), w1_words[0].bitcast(I32))
        for q in range(4):
            nc.sync.dma_start(
                w_scale_raw[32 * q : 32 * q + 4, :].bitcast(I32), w1_scales[0, 4 * q : 4 * q + 4, :].bitcast(I32)
            )
        nc.gpsimd.tensor_copy(
            w_word_dealt[:].rearrange("p (t m b) -> p t m b", t=PACK, b=2),
            w_word_raw[:].rearrange("p (m t b) -> p t m b", t=PACK, b=2),
        )
        nc.gpsimd.tensor_copy(
            w_scale_dealt[:].rearrange("p (t m) -> p t m", t=PACK),
            w_scale_raw[:].rearrange("p (m t) -> p t m", t=PACK),
        )

        z_codes = keep.tile([P, S], U32, name="z_codes", align_bytes=64)
        z_scales = keep.tile([P, S], U8, name="z_scales", align_bytes=64)
        early_sums2 = [psum.tile([P, LATE], F32, name="early_sums2_%d" % t, tag="bank%d" % (6 + t)) for t in range(2)]
        late_sums2 = {}
        h2_win = [keep.tile([P, S], F32, name="h2_win0", tag="even_tiles", align_bytes=64)]

        def second_product(t, lo, hi, sums):
            nc.tensor.matmul_mx(
                out=sums,
                lhsT=w_word_dealt[:, 2 * P * t : 2 * P * (t + 1)].bitcast(FP4X4),
                lhsT_scale=w_scale_dealt[:, P * t : P * (t + 1)],
                rhs=z_codes[:, lo:hi].bitcast(FP8X4),
                rhs_scale=z_scales[:, lo:hi],
                start=True,
                stop=True,
            )

        for c, (lo, hi) in enumerate(STRETCHES):
            width = hi - lo
            u = lo // HALF
            z_rows = keep.tile([P, PACK, width], BF16, name="z_rows%d" % c, align_bytes=64)
            for t in range(PACK):
                tag = "gate%d" % t if t > 0 else "gate0_%d" % c
                gate = keep.tile([P, width], F32, name="gate%d_%d" % (t, c), tag=tag, align_bytes=64)
                picked = gate_win[t][:].indirect(n1_list[:, lo // PER_COLUMN : hi // PER_COLUMN])
                if t == 0 or (t == 1 and c == 0):
                    nc.vector.tensor_copy(gate[:], picked)
                elif t < FIRST_TILES:
                    nc.scalar.activation(gate[:], picked, ACT.Copy)
                else:
                    nc.scalar.activation(gate[:], picked, ACT.Sigmoid, scale=H_FACTOR)
                nc.vector.scalar_tensor_tensor(
                    z_rows[:, t, :],
                    sums1[t, u][:, lo - HALF * u : hi - HALF * u],
                    scaled_gain[:, t : t + 1],
                    gate[:],
                    ALU.mult,
                    ALU.mult,
                )
            if c == LAST:
                warm = keep.tile([P, 1], F32, name="warm")
                nc.scalar.activation(warm[:], gate[:, 0:1], ACT.Sqrt, bias=quarter[:])
            tag = "odd_tiles" if c == LAST else "z_grouped%d" % c
            z_grouped = keep.tile([P, width, PACK], BF16, name="z_grouped%d" % c, tag=tag, align_bytes=64)
            nc.vector.tensor_copy(
                z_grouped[:].rearrange("p (c i) t -> p c t i", i=4),
                z_rows[:].rearrange("p t (c i) -> p c t i", i=4),
            )
            nc.vector.quantize_mx(
                out=z_codes[:, lo:hi].bitcast(FP8X4),
                scales=z_scales[:, lo:hi],
                in_=z_grouped[:].rearrange("p c t -> p (c t)"),
            )
            for t in range(FIRST_TILES):
                if c == LAST:
                    late_sums2[t] = psum.tile([P, width], F32, name="late_sums2_%d" % t, tag="bank%d" % (2 * t))
                second_product(t, lo, hi, late_sums2[t][:] if c == LAST else early_sums2[t][:, lo:hi])
            if hi == LATE:
                nc.scalar.copy(h2_win[0][:, 0:LATE], early_sums2[0][:])
        for t in range(FIRST_TILES, PACK):
            late_sums2[t] = psum.tile([P, S], F32, name="late_sums2_%d" % t, tag="bank%d" % (2 * t - 3))
            second_product(t, 0, S, late_sums2[t][:])

        out_rows = out_0.rearrange("(p t) c -> p t c", t=PACK)
        h2_win.append(keep.tile([P, S], F32, name="h2_win1", tag="odd_tiles", align_bytes=64))
        nc.vector.tensor_copy(h2_win[1][:, 0:LATE], early_sums2[1][:])
        for t in range(FIRST_TILES):
            nc.vector.tensor_copy(h2_win[t][:, LATE:S], late_sums2[t][:])
        pairs = []
        y_win = []
        for t in range(PACK):
            if t >= FIRST_TILES:
                tag = "even_tiles" if t % 2 == 0 else "odd_tiles"
                h2_win.append(keep.tile([P, S], F32, name="h2_win%d" % t, tag=tag, align_bytes=64))
                nc.scalar.copy(h2_win[t][:], late_sums2[t][:])
            pairs.append(keep.tile([P, S], F32, name="pair%d" % t, align_bytes=64))
            y_win.append(keep.tile([P, S], F32, name="y_win%d" % t, align_bytes=64))
            nc.scalar.activation(pairs[t][:, 0:HALF], h2_win[t][:].indirect(n2_list[:]), ACT.Copy, scale=-0.5)
            if t < FIRST_TILES:
                nc.vector.tensor_copy(pairs[t][:, HALF:S], h2_win[t][:].indirect(n3_list[:]))
            else:
                nc.scalar.activation(pairs[t][:, HALF:S], h2_win[t][:].indirect(n3_list[:]), ACT.Copy)
            nc.vector.tensor_tensor(y_win[t][:].indirect(n3_list[:]), pairs[t][:, 0:HALF], pairs[t][:, HALF:S], ALU.add)
        totals = []
        for t in range(PACK):
            squares = keep.tile([P, S], F32, name="squares%d" % t, align_bytes=64)
            totals.append(keep.tile([P, HALF], F32, name="total%d" % t, tag="total%d" % t, align_bytes=64))
            nc.scalar.activation(squares[:], pairs[t][:], ACT.Square)
            nc.vector.scalar_tensor_tensor(
                totals[t][:], squares[:, 0:HALF], 4.0, squares[:, HALF:S], ALU.mult, ALU.add
            )
        for t in range(PACK):
            root = keep.tile([P, HALF], F32, name="root%d" % t, align_bytes=64)
            nc.scalar.activation(root[:], totals[t][:], ACT.Sqrt, bias=quarter[:])
            nc.vector.tensor_copy(y_win[t][:].indirect(n2_list[:]), root[:])
            nc.sync.dma_start(out_rows[:, t, :], y_win[t][:])

        y_grouped = keep.tile([P, S, PACK], BF16, name="y_grouped", tag="total3", align_bytes=64)
        y_left = keep.tile([P, 2, HALF], BF16, name="y_left", tag="total2", align_bytes=64)
        y_codes = keep.tile([P, S], U32, name="y_codes", align_bytes=64)
        y_scales = keep.tile([P, S], U8, name="y_scales", align_bytes=64)
        for t in range(2):
            nc.scalar.copy(y_grouped[:, :, t], y_win[t][:])
        nc.scalar.copy(y_left[:, 0, :], y_win[2][:, 0:HALF])
        nc.scalar.copy(y_grouped[:, HALF:S, 2], y_win[2][:, HALF:S])
        nc.vector.tensor_copy(y_left[:, 1, :], y_win[3][:, 0:HALF])
        nc.scalar.copy(y_grouped[:, HALF:S, 3], y_win[3][:, HALF:S])
        nc.vector.tensor_copy(y_grouped[:, 0:HALF, 2:4], y_left[:].rearrange("p t c -> p c t"))
        words_out = out_1[0].rearrange("p n t -> p (n t)").bitcast(I32)
        for u in range(2):
            cols = slice(HALF * u, HALF * (u + 1))
            nc.vector.quantize_mx(
                out=y_codes[:, cols].bitcast(FP8X4),
                scales=y_scales[:, cols],
                in_=y_grouped[:, cols, :].rearrange("p c t -> p (c t)"),
            )
            nc.sync.dma_start(words_out[:, cols], y_codes[:, cols].bitcast(I32))
        for q in range(4):
            queue = nc.scalar if q % 2 == 0 else nc.sync
            queue.dma_start(out_2[0, 4 * q : 4 * q + 4, :].bitcast(I32), y_scales[32 * q : 32 * q + 4, :].bitcast(I32))
